import numpy as np
import ml_dtypes


def mxq(x, axis, fmt="e4m3"):
    dtype, down = {"e4m3": (ml_dtypes.float8_e4m3fn, 7), "e5m2": (ml_dtypes.float8_e5m2, 14)}[fmt]
    v = np.moveaxis(np.asarray(x, np.float32).astype(ml_dtypes.bfloat16).astype(np.float64), axis, -1)
    blocks = v.reshape(v.shape[:-1] + (-1, 32))
    amax = np.abs(blocks).max(-1, keepdims=True)
    byte = np.maximum(np.where(amax > 0, np.frexp(amax)[1] - 1 + 127, 0) - down, 1)
    scale = np.exp2(byte - 127.0)
    codes = (blocks / scale).astype(np.float32).astype(dtype).astype(np.float64)
    return np.moveaxis((codes * scale).reshape(v.shape), -1, axis)


WIDE = False


def mx_kscale(k):
    if not WIDE:
        return np.ones(k)
    levels = np.array([10, -10, 5, -5, 0])
    if k % 512:
        return np.exp2(np.random.permutation(np.resize(levels, k // 32))).repeat(32)
    a = np.empty((k // 512, 16))
    for p in range(k // 512):
        a[p, :8] = np.random.permutation(np.resize(levels, 8))
        for g in range(8):
            far = levels[np.abs(levels - a[p, g]) >= 10]
            a[p, g + 8] = far[np.random.randint(len(far))]
    return np.exp2(a.ravel()).repeat(32)


def f64(x):
    return np.asarray(x).astype(np.float64)


def striped(idx):
    return np.tile(idx.reshape(-1, 16).T, (8, 1)).astype(np.uint16)


def unstriped(offs):
    return offs[:16].T.reshape(-1).astype(np.int64)


E2M1 = np.array([0.0, 0.5, 1.0, 1.5, 2.0, 3.0, 4.0, 6.0, -0.0, -0.5, -1.0, -1.5, -2.0, -3.0, -4.0, -6.0])


def pack_weight(w, fmt):
    k, n = w.shape
    w = f64(np.asarray(w, np.float32).astype(ml_dtypes.bfloat16)).reshape(k // 32, 32, n)
    amax = np.abs(w).max(1)
    if fmt == "e4m3":
        byte = np.frexp(amax)[1] - 1 + 127 - 7
    else:
        mant, ex = np.frexp(amax / 6.0)
        byte = np.where(mant > 0.5, ex, ex - 1) + 127
    byte = np.clip(np.where(amax > 0, byte, 1), 1, 254)
    scaled = (w * np.exp2(127.0 - byte)[:, None, :]).reshape(k, n).astype(np.float32)
    by_word = np.ascontiguousarray(scaled.reshape(k // 512, 128, 4, n).transpose(0, 1, 3, 2))
    if fmt == "e4m3":
        words = by_word.astype(ml_dtypes.float8_e4m3fn).view(np.uint8)
    else:
        c = by_word.astype(ml_dtypes.float4_e2m1fn).view(np.uint8) & 0xF
        words = (c[..., 0::2] | (c[..., 1::2] << 4)).reshape(k // 512, 128, 2 * n)
    return np.ascontiguousarray(words), np.ascontiguousarray(byte.astype(np.uint8).reshape(k // 512, 16, n))


def unpack_weight(words, scales, fmt):
    g, _, n = scales.shape
    words = np.ascontiguousarray(words).reshape(g, 128, n, -1)
    if fmt == "e4m3":
        vals = words.view(ml_dtypes.float8_e4m3fn).astype(np.float64)
    else:
        nib = np.empty((g, 128, n, 4), np.uint8)
        nib[..., 0::2] = words & 0xF
        nib[..., 1::2] = words >> 4
        vals = E2M1[nib]
    vals = vals * np.repeat(np.exp2(scales.astype(np.float64) - 127.0), 8, axis=1)[..., None]
    return vals.transpose(0, 1, 3, 2).reshape(g * 512, n)


def gelu(v):
    return 0.5 * v * (1.0 + np.tanh(np.sqrt(2.0 / np.pi) * (v + 0.044715 * v**3)))


K, K2, H, N, S, P, T, TB = 1024, 512, 1024, 512, 1024, 512, 2048, 2048

def setup_inputs():
    n = np.random.standard_normal
    s, s2, u = mx_kscale(K)[:, None], mx_kscale(K2)[:, None], mx_kscale(H)[:, None]
    d = {}
    d["tab_words"], d["tab_scales"] = pack_weight(n((K, T)) * s, "e4m3")
    d["offs"] = striped(np.random.permutation(T)[:S])
    d["tab2_words"], d["tab2_scales"] = pack_weight(n((K2, TB)) * s2, "e4m3")
    d["offs2"] = striped(np.random.permutation(TB)[:P])
    d["pos1"] = striped(np.random.permutation(S)[:P])
    d["w1"] = (0.55 * n((K, H)) / K**0.5 / s).astype(np.float32)
    d["gain"] = (np.exp(0.3 * n(H)) * u[:, 0]).astype(np.float32)
    d["w2_words"], d["w2_scales"] = pack_weight(0.8 * n((K2, H)) / K2**0.5 / s2 * u.T, "e2m1")
    d["rig"] = np.exp(0.4 * n((H, P))).astype(np.float32)
    d["wgs"] = np.exp(0.3 * n((128, P))).astype(np.float32)
    d["w3"] = (0.9 * n((H, N)) / H**0.5 / u).astype(np.float32)
    d["target"] = (0.9 * n((N, S))).astype(np.float32)
    return d

def reference(tab_words, tab_scales, offs, tab2_words, tab2_scales, offs2, pos1, w1, gain, w2_words, w2_scales, rig, wgs, w3, target):
    v = unpack_weight(tab_words, tab_scales, "e4m3")[:, unstriped(offs)]
    v2 = unpack_weight(tab2_words, tab2_scales, "e4m3")[:, unstriped(offs2)]
    f = mxq(f64(w1), 0, "e4m3").T @ v
    a = (f + np.cos(f)) * f64(gain)[:, None]
    w2 = unpack_weight(w2_words, w2_scales, "e2m1")
    b = (w2.T @ v2) * f64(rig)
    placed = np.zeros((H, S))
    placed[:, unstriped(pos1)] = np.tile(f64(wgs), (H // 128, 1)) * b
    z = a + placed
    y = mxq(f64(w3), 0, "e4m3").T @ mxq(z, 0, "e4m3")
    return np.square(y - f64(target))

@@ -1,0 +1,272 @@
+import math
+from contextlib import ExitStack
+
+import concourse.mybir as mybir
+
+K, K2, H, N, S, NP, T = 1024, 512, 1024, 512, 1024, 512, 2048
+FLOPS = 2 * (K * H * S + K2 * H * NP + H * N * S)
+
+F32 = mybir.dt.float32
+BF16 = mybir.dt.bfloat16
+I32 = mybir.dt.int32
+U32 = mybir.dt.uint32
+U16 = mybir.dt.uint16
+U8 = mybir.dt.uint8
+FP8X4 = mybir.dt.float8_e4m3fn_x4
+FP4X4 = mybir.dt.float4_e2m1fn_x4
+ALU = mybir.AluOpType
+ACT = mybir.ActivationFunctionType
+
+P = 128
+PACK = 4
+PASS = P * PACK
+HALF = 512
+
+
+def tile_list_playground_hazard_misfit_kernel(
+    tc, tab_words, tab_scales, offs, tab2_words, tab2_scales, offs2, pos1, w1, gain,
+    w2_words, w2_scales, rig, wgs, w3, target, out,
+):
+    nc = tc.nc
+    with ExitStack() as ctx:
+        keep = ctx.enter_context(tc.tile_pool(name="keep", bufs=1))
+        ring = ctx.enter_context(tc.tile_pool(name="ring", bufs=2))
+        psum = ctx.enter_context(tc.psum_pool(name="psum", bufs=2))
+
+        offs_sb = keep.tile([P, S // 16], U16, name="offs_sb")
+        offs2_sb = keep.tile([P, NP // 16], U16, name="offs2_sb")
+        pos_sb = keep.tile([P, NP // 16], U16, name="pos_sb")
+        tab_sc = keep.tile([P, T], U8, name="tab_sc", align_bytes=64)
+        tab2_sc = keep.tile([P, T], U8, name="tab2_sc", align_bytes=64)
+        w2_sc_raw = keep.tile([P, H], U8, name="w2_sc_raw", align_bytes=64)
+        w2_raw = keep.tile([P, 2 * H], U8, name="w2_raw", align_bytes=64)
+        w2_codes = keep.tile([P, 2 * H], U8, name="w2_codes", align_bytes=64)
+        w2_sc = keep.tile([P, H], U8, name="w2_sc", align_bytes=64)
+        gain_sb = keep.tile([P, 2, PACK], F32, name="gain_sb")
+        wgs_sb = keep.tile([P, PACK, NP], F32, name="wgs_sb")
+        zero = keep.tile([P, 1], F32, name="zero")
+        zero_bias = keep.tile([P, 1], F32, name="zero_bias")
+        pages = [keep.tile([P, S], F32, name="page%d" % i) for i in range(8)]
+
+        nc.vector.memset(zero[:], 0.0)
+        nc.scalar.activation(zero_bias[:], zero[:], ACT.Sin)
+        for plane in (tab_sc, tab2_sc, w2_sc_raw):
+            nc.gpsimd.memset(plane[:].bitcast(I32), 0)
+        for page in pages:
+            nc.gpsimd.memset(page[:], 0.0)
+
+        def big(name):
+            return ring.tile([P, T], I32, name=name, tag="big", bufs=3, align_bytes=64)
+
+        nc.sync.dma_start(offs_sb[:], offs)
+        tabs = []
+        for a in range(2):
+            tab = big("tab%d" % a)
+            nc.sync.dma_start(tab[:], tab_words[a].rearrange("p n i -> p (n i)").bitcast(I32))
+            tabs.append(tab)
+        nc.sync.dma_start(offs2_sb[:], offs2)
+        tab2 = big("tab2")
+        nc.sync.dma_start(tab2[:], tab2_words[0].rearrange("p n i -> p (n i)").bitcast(I32))
+        nc.sync.dma_start(w2_raw[:].bitcast(I32), w2_words[0].bitcast(I32))
+        for q in range(4):
+            nc.scalar.dma_start(tab2_sc[32 * q : 32 * q + 4, :].bitcast(I32), tab2_scales[0, 4 * q : 4 * q + 4, :].bitcast(I32))
+        for q in range(4):
+            nc.scalar.dma_start(w2_sc_raw[32 * q : 32 * q + 4, :].bitcast(I32), w2_scales[0, 4 * q : 4 * q + 4, :].bitcast(I32))
+        for q in range(4):
+            nc.scalar.dma_start(tab_sc[32 * q : 32 * q + 8, :].bitcast(I32), tab_scales[:, 4 * q : 4 * q + 4, :].bitcast(I32))
+        nc.sync.dma_start(pos_sb[:], pos1)
+        nc.sync.dma_start(gain_sb[:], gain.rearrange("(g p t) -> p g t", g=2, t=PACK))
+        for q in range(4):
+            nc.sync.dma_start(wgs_sb[32 * q : 32 * q + 32, :, :], wgs.rearrange("(p t) j -> p t j", t=PACK))
+
+        rig_sb = {}
+
+        def load_rig(g, u):
+            tile = keep.tile([P, 2, NP], F32, name="rig%d%d" % (g, u))
+            rows = rig[g * PASS : (g + 1) * PASS, :].rearrange("(p t) j -> p t j", t=PACK)
+            nc.sync.dma_start(tile[:], rows[:, 2 * u : 2 * u + 2, :])
+            rig_sb[g, u] = tile
+
+        def load_weight(w, a, c):
+            raw = ring.tile([P, PACK, HALF], F32, name="w_raw", tag="w_raw", bufs=3)
+            rows = w[a * PASS : (a + 1) * PASS, c * HALF : (c + 1) * HALF]
+            nc.sync.dma_start(raw[:], rows.rearrange("(p i) c -> p i c", i=PACK))
+            return raw
+
+        load_rig(0, 0)
+        load_rig(0, 1)
+        w1_raw = {}
+        for g in range(2):
+            for a in range(2):
+                w1_raw[a, g] = load_weight(w1, a, g)
+        load_rig(1, 0)
+        load_rig(1, 1)
+
+        v_codes = []
+        for a in range(2):
+            codes = keep.tile([P, S], I32, name="v_codes%d" % a, align_bytes=64)
+            nc.vector.tensor_copy(codes[:].bitcast(U32), tabs[a][:].bitcast(U32).indirect(offs_sb[:]))
+            v_codes.append(codes)
+        nc.vector.tensor_copy(
+            w2_codes[:].rearrange("p (g t m b) -> p g m t b", g=2, t=PACK, b=2),
+            w2_raw[:].rearrange("p (g m t b) -> p g m t b", g=2, t=PACK, b=2),
+        )
+        nc.vector.tensor_copy(
+            w2_sc[:].rearrange("p (g t m) -> p g m t", g=2, t=PACK),
+            w2_sc_raw[:].rearrange("p (g m t) -> p g m t", g=2, t=PACK),
+        )
+        v2_codes = keep.tile([P, NP], I32, name="v2_codes", align_bytes=64)
+        nc.vector.tensor_copy(v2_codes[:].bitcast(U32), tab2[:].bitcast(U32).indirect(offs2_sb[:]))
+        v2_sc = keep.tile([P, NP], U8, name="v2_sc", align_bytes=64)
+        nc.vector.tensor_copy(v2_sc[:], tab2_sc[:].indirect(offs2_sb[:]))
+        v_sc = keep.tile([P, S], U8, name="v_sc", align_bytes=64)
+        nc.vector.tensor_copy(v_sc[:], tab_sc[:].indirect(offs_sb[:]))
+
+        def quantize(grouped, name, pool, bufs):
+            codes = pool.tile([P, HALF], I32, name=name + "_codes", bufs=bufs, align_bytes=64)
+            scales = pool.tile([P, HALF], U8, name=name + "_scales", bufs=bufs, align_bytes=64)
+            nc.vector.quantize_mx(out=codes[:].bitcast(FP8X4), scales=scales[:], in_=grouped[:])
+            return codes, scales
+
+        def grouped_tile():
+            return ring.tile([P, PACK * HALF], BF16, name="grouped", tag="grouped", bufs=3, align_bytes=64)
+
+        w1_q = {}
+
+        def prepare_w1(g):
+            for a in range(2):
+                grouped = grouped_tile()
+                nc.scalar.copy(
+                    grouped[:].rearrange("p (t m i) -> p m i t", t=PACK, i=PACK),
+                    w1_raw[a, g][:].rearrange("p i (m t) -> p m i t", t=PACK),
+                )
+                w1_q[a, g] = quantize(grouped, "w1_%d%d" % (a, g), keep, 1)
+
+        w3_q = {}
+
+        def prepare_w3(g):
+            raw = load_weight(w3, g, 0)
+            grouped = grouped_tile()
+            nc.scalar.copy(
+                grouped[:].rearrange("p (c i t) -> p c t i", t=PACK, i=4),
+                raw[:].rearrange("p t (c i) -> p c t i", i=4),
+            )
+            w3_q[g] = quantize(grouped, "w3_%d" % g, keep, 1)
+
+        def place(i):
+            g, t = divmod(i, PACK)
+            acc = psum.tile([P, NP], F32, name="b_acc", tag="b_acc", bufs=2)
+            nc.tensor.matmul_mx(
+                out=acc[:],
+                lhsT=w2_codes[:, 2 * P * i : 2 * P * (i + 1)].bitcast(FP4X4),
+                lhsT_scale=w2_sc[:, P * i : P * (i + 1)],
+                rhs=v2_codes[:].bitcast(FP8X4),
+                rhs_scale=v2_sc[:],
+                start=True,
+                stop=True,
+            )
+            b = ring.tile([P, NP], F32, name="b", tag="b", bufs=2)
+            nc.vector.tensor_tensor(b[:], acc[:], rig_sb[g, t // 2][:, t % 2, :], ALU.mult)
+            nc.vector.tensor_tensor(pages[i][:].indirect(pos_sb[:]), b[:], wgs_sb[:, t, :], ALU.mult)
+
+        feats = {}
+
+        def features(i, h):
+            g, t = divmod(i, PACK)
+            cols = slice(h * HALF, (h + 1) * HALF)
+            acc = psum.tile([P, HALF], F32, name="f_acc", tag="f_acc", bufs=4)
+            for a in range(2):
+                codes, scales = w1_q[a, g]
+                nc.tensor.matmul_mx(
+                    out=acc[:],
+                    lhsT=codes[:, P * t : P * (t + 1)].bitcast(FP8X4),
+                    lhsT_scale=scales[:, P * t : P * (t + 1)],
+                    rhs=v_codes[a][:, cols].bitcast(FP8X4),
+                    rhs_scale=v_sc[4 * a : P, cols],
+                    start=(a == 0),
+                    stop=(a == 1),
+                )
+            feat = ring.tile([P, HALF], F32, name="feat", tag="feat", bufs=10)
+            nc.scalar.activation(feat[:], acc[:], ACT.Abs, bias=zero_bias[:])
+            nc.scalar.activation(feat[:], feat[:], ACT.Sin, bias=math.pi / 2, scale=-1.0)
+            nc.vector.tensor_tensor(feat[:], acc[:], feat[:], ALU.add)
+            feats[i, h] = feat
+
+        z_rows = {}
+
+        def combine(i, h):
+            g, t = divmod(i, PACK)
+            if t == 0:
+                z_rows[g, h] = ring.tile([P, PACK, HALF], BF16, name="z_rows", tag="z_rows", bufs=3)
+            nc.vector.scalar_tensor_tensor(
+                out=z_rows[g, h][:, t, :],
+                in0=feats[i, h][:],
+                scalar=gain_sb[:, g, t : t + 1],
+                in1=pages[i][:, h * HALF : (h + 1) * HALF],
+                op0=ALU.mult,
+                op1=ALU.add,
+            )
+
+        z_q = {}
+
+        def prepare_z(g, h):
+            grouped = grouped_tile()
+            nc.scalar.copy(
+                grouped[:].rearrange("p (c i t) -> p c t i", t=PACK, i=4),
+                z_rows[g, h][:].rearrange("p t (c i) -> p c t i", i=4),
+            )
+            z_q[g, h] = quantize(grouped, "z", ring, 4)
+
+        target_sb = {}
+
+        def load_target(h):
+            tile = big("target%d" % h)
+            view = tile[:].bitcast(F32).rearrange("p (q j) -> p q j", q=4)
+            nc.sync.dma_start(view, target[:, h * HALF : (h + 1) * HALF].rearrange("(q p) j -> p q j", p=P))
+            target_sb[h] = view
+
+        def misfit(q, h):
+            acc = psum.tile([P, HALF], F32, name="y_acc", tag="y_acc", bufs=2)
+            for g in range(2):
+                w_codes, w_scales = w3_q[g]
+                z_codes, z_scales = z_q[g, h]
+                nc.tensor.matmul_mx(
+                    out=acc[:],
+                    lhsT=w_codes[:, P * q : P * (q + 1)].bitcast(FP8X4),
+                    lhsT_scale=w_scales[:, P * q : P * (q + 1)],
+                    rhs=z_codes[:].bitcast(FP8X4),
+                    rhs_scale=z_scales[:],
+                    start=(g == 0),
+                    stop=(g == 1),
+                )
+            diff = ring.tile([P, HALF], F32, name="diff", tag="diff", bufs=4)
+            nc.vector.tensor_tensor(diff[:], acc[:], target_sb[h][:, q, :], ALU.subtract)
+            nc.scalar.activation(diff[:], diff[:], ACT.Square)
+            nc.sync.dma_start(out[q * P : (q + 1) * P, h * HALF : (h + 1) * HALF], diff[:])
+
+        place(0)
+        place(1)
+        prepare_w1(0)
+        for i in range(8):
+            if i + 2 < 8:
+                place(i + 2)
+            features(i, 0)
+            features(i, 1)
+            combine(i, 0)
+            if i < PACK:
+                combine(i, 1)
+            if i == 0:
+                prepare_w1(1)
+            if i == 3:
+                prepare_z(0, 0)
+                prepare_z(0, 1)
+            if i in (4, 5):
+                prepare_w3(i - 4)
+                load_target(i - 4)
+        prepare_z(1, 0)
+        for i in range(PACK, 8):
+            combine(i, 1)
+        prepare_z(1, 1)
+        for h in range(2):
+            for q in range(4):
+                misfit(q, h)

@@ -2,6 +2,7 @@ import math
 from contextlib import ExitStack
 
 import concourse.mybir as mybir
+from concourse.masks import make_identity
 
 K, K2, H, N, S, NP, T = 1024, 512, 1024, 512, 1024, 512, 2048
 FLOPS = 2 * (K * H * S + K2 * H * NP + H * N * S)
@@ -21,6 +22,7 @@ P = 128
 PACK = 4
 PASS = P * PACK
 HALF = 512
+PAGES = 6
 
 
 def tile_list_playground_hazard_misfit_kernel(
@@ -44,40 +46,30 @@ def tile_list_playground_hazard_misfit_kernel(
         w2_sc = keep.tile([P, H], U8, name="w2_sc", align_bytes=64)
         gain_sb = keep.tile([P, 2, PACK], F32, name="gain_sb")
         wgs_sb = keep.tile([P, PACK, NP], F32, name="wgs_sb")
+        ident = keep.tile([P, P], F32, name="ident")
         zero = keep.tile([P, 1], F32, name="zero")
         zero_bias = keep.tile([P, 1], F32, name="zero_bias")
-        pages = [keep.tile([P, S], F32, name="page%d" % i) for i in range(8)]
+        pages = [keep.tile([P, S], F32, name="page%d" % i) for i in range(PAGES)]
 
+        nc.gpsimd.memset(tab_sc[:].bitcast(I32), 0)
+        nc.gpsimd.memset(w2_sc_raw[:].bitcast(I32), 0)
+        nc.vector.memset(tab2_sc[:].bitcast(I32), 0)
         nc.vector.memset(zero[:], 0.0)
         nc.scalar.activation(zero_bias[:], zero[:], ACT.Sin)
-        for plane in (tab_sc, tab2_sc, w2_sc_raw):
-            nc.gpsimd.memset(plane[:].bitcast(I32), 0)
         for page in pages:
             nc.gpsimd.memset(page[:], 0.0)
+        make_identity(nc, ident[:])
+
+        banks = [[psum.tile([P, HALF], F32, name="bank%d%d" % (h, t), bufs=1) for t in range(4)] for h in range(2)]
 
         def big(name):
             return ring.tile([P, T], I32, name=name, tag="big", bufs=3, align_bytes=64)
 
-        nc.sync.dma_start(offs_sb[:], offs)
-        tabs = []
-        for a in range(2):
-            tab = big("tab%d" % a)
-            nc.sync.dma_start(tab[:], tab_words[a].rearrange("p n i -> p (n i)").bitcast(I32))
-            tabs.append(tab)
-        nc.sync.dma_start(offs2_sb[:], offs2)
-        tab2 = big("tab2")
-        nc.sync.dma_start(tab2[:], tab2_words[0].rearrange("p n i -> p (n i)").bitcast(I32))
-        nc.sync.dma_start(w2_raw[:].bitcast(I32), w2_words[0].bitcast(I32))
-        for q in range(4):
-            nc.scalar.dma_start(tab2_sc[32 * q : 32 * q + 4, :].bitcast(I32), tab2_scales[0, 4 * q : 4 * q + 4, :].bitcast(I32))
-        for q in range(4):
-            nc.scalar.dma_start(w2_sc_raw[32 * q : 32 * q + 4, :].bitcast(I32), w2_scales[0, 4 * q : 4 * q + 4, :].bitcast(I32))
-        for q in range(4):
-            nc.scalar.dma_start(tab_sc[32 * q : 32 * q + 8, :].bitcast(I32), tab_scales[:, 4 * q : 4 * q + 4, :].bitcast(I32))
-        nc.sync.dma_start(pos_sb[:], pos1)
-        nc.sync.dma_start(gain_sb[:], gain.rearrange("(g p t) -> p g t", g=2, t=PACK))
-        for q in range(4):
-            nc.sync.dma_start(wgs_sb[32 * q : 32 * q + 32, :, :], wgs.rearrange("(p t) j -> p t j", t=PACK))
+        def load_weight(w, a, c):
+            raw = ring.tile([P, PACK, HALF], F32, name="w_raw", tag="w_raw", bufs=4)
+            rows = w[a * PASS : (a + 1) * PASS, c * HALF : (c + 1) * HALF]
+            nc.sync.dma_start(raw[:], rows.rearrange("(p i) c -> p i c", i=PACK))
+            return raw
 
         rig_sb = {}
 
@@ -87,44 +79,70 @@ def tile_list_playground_hazard_misfit_kernel(
             nc.sync.dma_start(tile[:], rows[:, 2 * u : 2 * u + 2, :])
             rig_sb[g, u] = tile
 
-        def load_weight(w, a, c):
-            raw = ring.tile([P, PACK, HALF], F32, name="w_raw", tag="w_raw", bufs=3)
-            rows = w[a * PASS : (a + 1) * PASS, c * HALF : (c + 1) * HALF]
-            nc.sync.dma_start(raw[:], rows.rearrange("(p i) c -> p i c", i=PACK))
-            return raw
+        def load_target(h):
+            view = ring.tile([P, 4, HALF], F32, name="target_sb", tag="w_raw", bufs=4)[:]
+            nc.sync.dma_start(view, target[:, h * HALF : (h + 1) * HALF].rearrange("(q p) j -> p q j", p=P))
+            target_sb[h] = view
 
+        w1_raw = {}
+        w3_raw = []
+        target_sb = {}
+        tabs = []
+        nc.sync.dma_start(offs_sb[:], offs)
+        tabs.append(big("tab0"))
+        nc.sync.dma_start(tabs[0][:], tab_words[0].rearrange("p n i -> p (n i)").bitcast(I32))
+        tabs.append(big("tab1"))
+        nc.sync.dma_start(tabs[1][:], tab_words[1].rearrange("p n i -> p (n i)").bitcast(I32))
+        nc.sync.dma_start(offs2_sb[:], offs2)
+        nc.sync.dma_start(pos_sb[:], pos1)
+        nc.sync.dma_start(gain_sb[:], gain.rearrange("(g p t) -> p g t", g=2, t=PACK))
+        nc.sync.dma_start(w2_raw[:].bitcast(I32), w2_words[0].bitcast(I32))
+        tab2 = big("tab2")
+        nc.sync.dma_start(tab2[:], tab2_words[0].rearrange("p n i -> p (n i)").bitcast(I32))
+        for q in range(4):
+            nc.sync.dma_start(tab_sc[32 * q : 32 * q + 8, :].bitcast(I32), tab_scales[:, 4 * q : 4 * q + 4, :].bitcast(I32))
+        w1_raw[0, 0] = load_weight(w1, 0, 0)
+        for q in range(4):
+            nc.sync.dma_start(tab2_sc[32 * q : 32 * q + 4, :].bitcast(I32), tab2_scales[0, 4 * q : 4 * q + 4, :].bitcast(I32))
+        w1_raw[1, 0] = load_weight(w1, 1, 0)
+        for q in range(4):
+            nc.sync.dma_start(w2_sc_raw[32 * q : 32 * q + 4, :].bitcast(I32), w2_scales[0, 4 * q : 4 * q + 4, :].bitcast(I32))
+        w1_raw[0, 1] = load_weight(w1, 0, 1)
+        w1_raw[1, 1] = load_weight(w1, 1, 1)
+        for q in (0, 2, 1, 3):
+            nc.sync.dma_start(wgs_sb[32 * q : 32 * q + 32, :, :], wgs.rearrange("(p t) j -> p t j", t=PACK))
         load_rig(0, 0)
         load_rig(0, 1)
-        w1_raw = {}
-        for g in range(2):
-            for a in range(2):
-                w1_raw[a, g] = load_weight(w1, a, g)
         load_rig(1, 0)
         load_rig(1, 1)
+        w3_raw.append(load_weight(w3, 0, 0))
+        w3_raw.append(load_weight(w3, 1, 0))
+        load_target(0)
+        load_target(1)
 
         v_codes = []
         for a in range(2):
             codes = keep.tile([P, S], I32, name="v_codes%d" % a, align_bytes=64)
             nc.vector.tensor_copy(codes[:].bitcast(U32), tabs[a][:].bitcast(U32).indirect(offs_sb[:]))
             v_codes.append(codes)
-        nc.vector.tensor_copy(
-            w2_codes[:].rearrange("p (g t m b) -> p g m t b", g=2, t=PACK, b=2),
-            w2_raw[:].rearrange("p (g m t b) -> p g m t b", g=2, t=PACK, b=2),
-        )
-        nc.vector.tensor_copy(
-            w2_sc[:].rearrange("p (g t m) -> p g m t", g=2, t=PACK),
-            w2_sc_raw[:].rearrange("p (g m t) -> p g m t", g=2, t=PACK),
-        )
+        v_sc = keep.tile([P, S], U8, name="v_sc", align_bytes=64)
+        nc.vector.tensor_copy(v_sc[:], tab_sc[:].indirect(offs_sb[:]))
         v2_codes = keep.tile([P, NP], I32, name="v2_codes", align_bytes=64)
         nc.vector.tensor_copy(v2_codes[:].bitcast(U32), tab2[:].bitcast(U32).indirect(offs2_sb[:]))
         v2_sc = keep.tile([P, NP], U8, name="v2_sc", align_bytes=64)
         nc.vector.tensor_copy(v2_sc[:], tab2_sc[:].indirect(offs2_sb[:]))
-        v_sc = keep.tile([P, S], U8, name="v_sc", align_bytes=64)
-        nc.vector.tensor_copy(v_sc[:], tab_sc[:].indirect(offs_sb[:]))
+        nc.vector.tensor_copy(
+            w2_codes[:].rearrange("p (g t m b) -> p g t m b", g=2, t=PACK, b=2),
+            w2_raw[:].rearrange("p (g m t b) -> p g t m b", g=2, t=PACK, b=2),
+        )
+        nc.vector.tensor_copy(
+            w2_sc[:].rearrange("p (g t m) -> p g t m", g=2, t=PACK),
+            w2_sc_raw[:].rearrange("p (g m t) -> p g t m", g=2, t=PACK),
+        )
 
-        def quantize(grouped, name, pool, bufs):
-            codes = pool.tile([P, HALF], I32, name=name + "_codes", bufs=bufs, align_bytes=64)
-            scales = pool.tile([P, HALF], U8, name=name + "_scales", bufs=bufs, align_bytes=64)
+        def quantize(grouped):
+            codes = ring.tile([P, HALF], I32, name="codes", tag="codes", bufs=6, align_bytes=64)
+            scales = ring.tile([P, HALF], U8, name="scales", tag="scales", bufs=6, align_bytes=64)
             nc.vector.quantize_mx(out=codes[:].bitcast(FP8X4), scales=scales[:], in_=grouped[:])
             return codes, scales
 
@@ -140,22 +158,27 @@ def tile_list_playground_hazard_misfit_kernel(
                     grouped[:].rearrange("p (t m i) -> p m i t", t=PACK, i=PACK),
                     w1_raw[a, g][:].rearrange("p i (m t) -> p m i t", t=PACK),
                 )
-                w1_q[a, g] = quantize(grouped, "w1_%d%d" % (a, g), keep, 1)
+                w1_q[a, g] = quantize(grouped)
 
         w3_q = {}
 
         def prepare_w3(g):
-            raw = load_weight(w3, g, 0)
+            raw = w3_raw[g]
             grouped = grouped_tile()
             nc.scalar.copy(
                 grouped[:].rearrange("p (c i t) -> p c t i", t=PACK, i=4),
                 raw[:].rearrange("p t (c i) -> p c t i", i=4),
             )
-            w3_q[g] = quantize(grouped, "w3_%d" % g, keep, 1)
+            w3_q[g] = quantize(grouped)
 
-        def place(i):
+        def page_of(i):
+            return pages[i] if i < PAGES else pages[PAGES + 3 - i]
+
+        weighted = {}
+
+        def weigh(i):
             g, t = divmod(i, PACK)
-            acc = psum.tile([P, NP], F32, name="b_acc", tag="b_acc", bufs=2)
+            acc = banks[g][t]
             nc.tensor.matmul_mx(
                 out=acc[:],
                 lhsT=w2_codes[:, 2 * P * i : 2 * P * (i + 1)].bitcast(FP4X4),
@@ -165,44 +188,66 @@ def tile_list_playground_hazard_misfit_kernel(
                 start=True,
                 stop=True,
             )
-            b = ring.tile([P, NP], F32, name="b", tag="b", bufs=2)
-            nc.vector.tensor_tensor(b[:], acc[:], rig_sb[g, t // 2][:, t % 2, :], ALU.mult)
-            nc.vector.tensor_tensor(pages[i][:].indirect(pos_sb[:]), b[:], wgs_sb[:, t, :], ALU.mult)
+            if t == 0:
+                weighted[g] = big("b%d" % g)[:].bitcast(F32).rearrange("p (t j) -> p t j", t=PACK)
+            nc.vector.tensor_tensor(weighted[g][:, t, :], acc[:], wgs_sb[:, t, :], ALU.mult)
 
-        feats = {}
-
-        def features(i, h):
+        def place(i):
             g, t = divmod(i, PACK)
-            cols = slice(h * HALF, (h + 1) * HALF)
-            acc = psum.tile([P, HALF], F32, name="f_acc", tag="f_acc", bufs=4)
-            for a in range(2):
-                codes, scales = w1_q[a, g]
-                nc.tensor.matmul_mx(
-                    out=acc[:],
-                    lhsT=codes[:, P * t : P * (t + 1)].bitcast(FP8X4),
-                    lhsT_scale=scales[:, P * t : P * (t + 1)],
-                    rhs=v_codes[a][:, cols].bitcast(FP8X4),
-                    rhs_scale=v_sc[4 * a : P, cols],
-                    start=(a == 0),
-                    stop=(a == 1),
-                )
-            feat = ring.tile([P, HALF], F32, name="feat", tag="feat", bufs=10)
-            nc.scalar.activation(feat[:], acc[:], ACT.Abs, bias=zero_bias[:])
-            nc.scalar.activation(feat[:], feat[:], ACT.Sin, bias=math.pi / 2, scale=-1.0)
-            nc.vector.tensor_tensor(feat[:], acc[:], feat[:], ALU.add)
-            feats[i, h] = feat
+            nc.vector.tensor_tensor(page_of(i)[:].indirect(pos_sb[:]), weighted[g][:, t, :], rig_sb[g, t // 2][:, t % 2, :], ALU.mult)
+
+        f_t = {}
+
+        def products(g, h):
+            f_t[g, h] = ring.tile([P, 4, HALF], F32, name="f_t", tag="f_t", bufs=4)
+            for c in range(4):
+                cols = slice(h * HALF + c * P, h * HALF + (c + 1) * P)
+                acc = banks[0 if (g, h) == (0, 0) else 1][c]
+                for a in range(2):
+                    codes, scales = w1_q[a, g]
+                    nc.tensor.matmul_mx(
+                        out=acc[:],
+                        lhsT=v_codes[a][:, cols].bitcast(FP8X4),
+                        lhsT_scale=v_sc[4 * a : P, cols],
+                        rhs=codes[:].bitcast(FP8X4),
+                        rhs_scale=scales[:],
+                        start=(a == 0),
+                        stop=(a == 1),
+                    )
+                nc.scalar.copy(f_t[g, h][:, c, :], acc[:])
+
+        cos_t = {}
+        scratch = [keep.tile([P, 2, HALF], F32, name="scratch%d" % u, align_bytes=64) for u in range(2)]
+
+        def cosines(g, h):
+            cos_t[g, h] = ring.tile([P, 4, HALF], F32, name="cos_t", tag="cos_t", bufs=3)
+            for u in range(2):
+                nc.scalar.activation(scratch[u][:], f_t[g, h][:, 2 * u : 2 * u + 2, :], ACT.Abs, bias=zero_bias[:])
+            for u in range(2):
+                nc.scalar.activation(cos_t[g, h][:, 2 * u : 2 * u + 2, :], scratch[u][:], ACT.Sin, bias=math.pi / 2, scale=-1.0)
 
         z_rows = {}
 
         def combine(i, h):
             g, t = divmod(i, PACK)
             if t == 0:
-                z_rows[g, h] = ring.tile([P, PACK, HALF], BF16, name="z_rows", tag="z_rows", bufs=3)
+                z_rows[g, h] = ring.tile([P, PACK, HALF], BF16, name="z_rows", tag="z_rows", bufs=4)
+            total = banks[h][t]
+            for c in range(4):
+                for n, term in enumerate((cos_t[g, h], f_t[g, h])):
+                    nc.tensor.matmul(
+                        total[:, c * P : (c + 1) * P],
+                        lhsT=term[:, c, t * P : (t + 1) * P],
+                        rhs=ident[:],
+                        start=(n == 0),
+                        stop=(n == 1),
+                        is_transpose=True,
+                    )
             nc.vector.scalar_tensor_tensor(
                 out=z_rows[g, h][:, t, :],
-                in0=feats[i, h][:],
+                in0=total[:],
                 scalar=gain_sb[:, g, t : t + 1],
-                in1=pages[i][:, h * HALF : (h + 1) * HALF],
+                in1=page_of(i)[:, h * HALF : (h + 1) * HALF],
                 op0=ALU.mult,
                 op1=ALU.add,
             )
@@ -210,24 +255,21 @@ def tile_list_playground_hazard_misfit_kernel(
         z_q = {}
 
         def prepare_z(g, h):
-            grouped = grouped_tile()
+            if g == 0:
+                grouped = scratch[h][:].rearrange("p c r -> p (c r)").bitcast(BF16)
+            else:
+                grouped = grouped_tile()
             nc.scalar.copy(
                 grouped[:].rearrange("p (c i t) -> p c t i", t=PACK, i=4),
                 z_rows[g, h][:].rearrange("p t (c i) -> p c t i", i=4),
             )
-            z_q[g, h] = quantize(grouped, "z", ring, 4)
+            z_q[g, h] = quantize(grouped)
 
-        target_sb = {}
-
-        def load_target(h):
-            tile = big("target%d" % h)
-            view = tile[:].bitcast(F32).rearrange("p (q j) -> p q j", q=4)
-            nc.sync.dma_start(view, target[:, h * HALF : (h + 1) * HALF].rearrange("(q p) j -> p q j", p=P))
-            target_sb[h] = view
+        diffs = {}
 
         def misfit(q, h):
-            acc = psum.tile([P, HALF], F32, name="y_acc", tag="y_acc", bufs=2)
-            for g in range(2):
+            acc = banks[h][q]
+            for g in (1, 0):
                 w_codes, w_scales = w3_q[g]
                 z_codes, z_scales = z_q[g, h]
                 nc.tensor.matmul_mx(
@@ -236,36 +278,43 @@ def tile_list_playground_hazard_misfit_kernel(
                     lhsT_scale=w_scales[:, P * q : P * (q + 1)],
                     rhs=z_codes[:].bitcast(FP8X4),
                     rhs_scale=z_scales[:],
-                    start=(g == 0),
-                    stop=(g == 1),
+                    start=(g == 1),
+                    stop=(g == 0),
                 )
-            diff = ring.tile([P, HALF], F32, name="diff", tag="diff", bufs=4)
-            nc.vector.tensor_tensor(diff[:], acc[:], target_sb[h][:, q, :], ALU.subtract)
-            nc.scalar.activation(diff[:], diff[:], ACT.Square)
-            nc.sync.dma_start(out[q * P : (q + 1) * P, h * HALF : (h + 1) * HALF], diff[:])
+            if q == 0:
+                diffs[h] = ring.tile([P, 4, HALF], F32, name="diff", tag="f_t", bufs=4)
+            diff = diffs[h][:, q, :]
+            nc.vector.tensor_tensor(diff, acc[:], target_sb[h][:, q, :], ALU.subtract)
+            nc.scalar.activation(diff, diff, ACT.Square)
+            nc.sync.dma_start(out[q * P : (q + 1) * P, h * HALF : (h + 1) * HALF], diff)
 
-        place(0)
-        place(1)
         prepare_w1(0)
+        prepare_w1(1)
         for i in range(8):
-            if i + 2 < 8:
-                place(i + 2)
-            features(i, 0)
-            features(i, 1)
-            combine(i, 0)
-            if i < PACK:
-                combine(i, 1)
-            if i == 0:
-                prepare_w1(1)
-            if i == 3:
-                prepare_z(0, 0)
-                prepare_z(0, 1)
-            if i in (4, 5):
-                prepare_w3(i - 4)
-                load_target(i - 4)
+            weigh(i)
+        for i in range(PAGES):
+            place(i)
+        products(0, 0)
+        products(0, 1)
+        cosines(0, 0)
+        products(1, 0)
+        products(1, 1)
+        cosines(0, 1)
+        cosines(1, 0)
+        cosines(1, 1)
+        for h in range(2):
+            for t in range(PACK):
+                combine(t, h)
+        for i in range(PAGES, 8):
+            place(i)
+        for h in range(2):
+            for t in range(PACK):
+                combine(PACK + t, h)
+        for g in range(2):
+            prepare_w3(g)
+        prepare_z(0, 0)
+        prepare_z(0, 1)
         prepare_z(1, 0)
-        for i in range(PACK, 8):
-            combine(i, 1)
         prepare_z(1, 1)
         for h in range(2):
             for q in range(4):

@@ -95,19 +95,18 @@ def tile_list_playground_hazard_misfit_kernel(
         nc.sync.dma_start(tabs[1][:], tab_words[1].rearrange("p n i -> p (n i)").bitcast(I32))
         nc.sync.dma_start(offs2_sb[:], offs2)
         nc.sync.dma_start(pos_sb[:], pos1)
-        nc.sync.dma_start(gain_sb[:], gain.rearrange("(g p t) -> p g t", g=2, t=PACK))
         nc.sync.dma_start(w2_raw[:].bitcast(I32), w2_words[0].bitcast(I32))
+        w1_raw[0, 0] = load_weight(w1, 0, 0)
         tab2 = big("tab2")
         nc.sync.dma_start(tab2[:], tab2_words[0].rearrange("p n i -> p (n i)").bitcast(I32))
         for q in range(4):
             nc.sync.dma_start(tab_sc[32 * q : 32 * q + 8, :].bitcast(I32), tab_scales[:, 4 * q : 4 * q + 4, :].bitcast(I32))
-        w1_raw[0, 0] = load_weight(w1, 0, 0)
-        for q in range(4):
-            nc.sync.dma_start(tab2_sc[32 * q : 32 * q + 4, :].bitcast(I32), tab2_scales[0, 4 * q : 4 * q + 4, :].bitcast(I32))
         w1_raw[1, 0] = load_weight(w1, 1, 0)
         for q in range(4):
-            nc.sync.dma_start(w2_sc_raw[32 * q : 32 * q + 4, :].bitcast(I32), w2_scales[0, 4 * q : 4 * q + 4, :].bitcast(I32))
+            nc.sync.dma_start(tab2_sc[32 * q : 32 * q + 4, :].bitcast(I32), tab2_scales[0, 4 * q : 4 * q + 4, :].bitcast(I32))
         w1_raw[0, 1] = load_weight(w1, 0, 1)
+        for q in range(4):
+            nc.sync.dma_start(w2_sc_raw[32 * q : 32 * q + 4, :].bitcast(I32), w2_scales[0, 4 * q : 4 * q + 4, :].bitcast(I32))
         w1_raw[1, 1] = load_weight(w1, 1, 1)
         for q in (0, 2, 1, 3):
             nc.sync.dma_start(wgs_sb[32 * q : 32 * q + 32, :, :], wgs.rearrange("(p t) j -> p t j", t=PACK))
@@ -115,6 +114,7 @@ def tile_list_playground_hazard_misfit_kernel(
         load_rig(0, 1)
         load_rig(1, 0)
         load_rig(1, 1)
+        nc.sync.dma_start(gain_sb[:], gain.rearrange("(g p t) -> p g t", g=2, t=PACK))
         w3_raw.append(load_weight(w3, 0, 0))
         w3_raw.append(load_weight(w3, 1, 0))
         load_target(0)
@@ -155,8 +155,8 @@ def tile_list_playground_hazard_misfit_kernel(
             for a in range(2):
                 grouped = grouped_tile()
                 nc.scalar.copy(
-                    grouped[:].rearrange("p (t m i) -> p m i t", t=PACK, i=PACK),
-                    w1_raw[a, g][:].rearrange("p i (m t) -> p m i t", t=PACK),
+                    grouped[:].rearrange("p (c i t) -> p c t i", t=PACK, i=4),
+                    w1_raw[a, g][:].rearrange("p t (c i) -> p c t i", i=4),
                 )
                 w1_q[a, g] = quantize(grouped)
 
@@ -214,7 +214,10 @@ def tile_list_playground_hazard_misfit_kernel(
                         start=(a == 0),
                         stop=(a == 1),
                     )
-                nc.scalar.copy(f_t[g, h][:, c, :], acc[:])
+                nc.scalar.copy(
+                    f_t[g, h][:, c, :].rearrange("p (t m) -> p t m", t=PACK),
+                    acc[:].rearrange("p (m t) -> p t m", t=PACK),
+                )
 
         cos_t = {}
         scratch = [keep.tile([P, 2, HALF], F32, name="scratch%d" % u, align_bytes=64) for u in range(2)]
@@ -269,7 +272,7 @@ def tile_list_playground_hazard_misfit_kernel(
 
         def misfit(q, h):
             acc = banks[h][q]
-            for g in (1, 0):
+            for g in (h, 1 - h):
                 w_codes, w_scales = w3_q[g]
                 z_codes, z_scales = z_q[g, h]
                 nc.tensor.matmul_mx(
@@ -278,8 +281,8 @@ def tile_list_playground_hazard_misfit_kernel(
                     lhsT_scale=w_scales[:, P * q : P * (q + 1)],
                     rhs=z_codes[:].bitcast(FP8X4),
                     rhs_scale=z_scales[:],
-                    start=(g == 1),
-                    stop=(g == 0),
+                    start=(g == h),
+                    stop=(g != h),
                 )
             if q == 0:
                 diffs[h] = ring.tile([P, 4, HALF], F32, name="diff", tag="f_t", bufs=4)
@@ -312,8 +315,7 @@ def tile_list_playground_hazard_misfit_kernel(
                 combine(PACK + t, h)
         for g in range(2):
             prepare_w3(g)
-        prepare_z(0, 0)
-        prepare_z(0, 1)
+            prepare_z(0, g)
         prepare_z(1, 0)
         prepare_z(1, 1)
         for h in range(2):

@@ -66,7 +66,7 @@ def tile_list_playground_hazard_misfit_kernel(
             return ring.tile([P, T], I32, name=name, tag="big", bufs=3, align_bytes=64)
 
         def load_weight(w, a, c):
-            raw = ring.tile([P, PACK, HALF], F32, name="w_raw", tag="w_raw", bufs=4)
+            raw = ring.tile([P, PACK, HALF], F32, name="w_raw", tag="w_raw", bufs=5, align_bytes=64)
             rows = w[a * PASS : (a + 1) * PASS, c * HALF : (c + 1) * HALF]
             nc.sync.dma_start(raw[:], rows.rearrange("(p i) c -> p i c", i=PACK))
             return raw
@@ -80,7 +80,7 @@ def tile_list_playground_hazard_misfit_kernel(
             rig_sb[g, u] = tile
 
         def load_target(h):
-            view = ring.tile([P, 4, HALF], F32, name="target_sb", tag="w_raw", bufs=4)[:]
+            view = ring.tile([P, 4, HALF], F32, name="target_sb", tag="w_raw", bufs=5, align_bytes=64)[:]
             nc.sync.dma_start(view, target[:, h * HALF : (h + 1) * HALF].rearrange("(q p) j -> p q j", p=P))
             target_sb[h] = view
 
@@ -95,26 +95,26 @@ def tile_list_playground_hazard_misfit_kernel(
         nc.sync.dma_start(tabs[1][:], tab_words[1].rearrange("p n i -> p (n i)").bitcast(I32))
         nc.sync.dma_start(offs2_sb[:], offs2)
         nc.sync.dma_start(pos_sb[:], pos1)
+        nc.sync.dma_start(gain_sb[:], gain.rearrange("(g p t) -> p g t", g=2, t=PACK))
         nc.sync.dma_start(w2_raw[:].bitcast(I32), w2_words[0].bitcast(I32))
         w1_raw[0, 0] = load_weight(w1, 0, 0)
-        tab2 = big("tab2")
-        nc.sync.dma_start(tab2[:], tab2_words[0].rearrange("p n i -> p (n i)").bitcast(I32))
         for q in range(4):
             nc.sync.dma_start(tab_sc[32 * q : 32 * q + 8, :].bitcast(I32), tab_scales[:, 4 * q : 4 * q + 4, :].bitcast(I32))
         w1_raw[1, 0] = load_weight(w1, 1, 0)
         for q in range(4):
             nc.sync.dma_start(tab2_sc[32 * q : 32 * q + 4, :].bitcast(I32), tab2_scales[0, 4 * q : 4 * q + 4, :].bitcast(I32))
-        w1_raw[0, 1] = load_weight(w1, 0, 1)
+        tab2 = big("tab2")
+        nc.sync.dma_start(tab2[:], tab2_words[0].rearrange("p n i -> p (n i)").bitcast(I32))
         for q in range(4):
             nc.sync.dma_start(w2_sc_raw[32 * q : 32 * q + 4, :].bitcast(I32), w2_scales[0, 4 * q : 4 * q + 4, :].bitcast(I32))
-        w1_raw[1, 1] = load_weight(w1, 1, 1)
         for q in (0, 2, 1, 3):
             nc.sync.dma_start(wgs_sb[32 * q : 32 * q + 32, :, :], wgs.rearrange("(p t) j -> p t j", t=PACK))
+        w1_raw[0, 1] = load_weight(w1, 0, 1)
+        w1_raw[1, 1] = load_weight(w1, 1, 1)
         load_rig(0, 0)
         load_rig(0, 1)
         load_rig(1, 0)
         load_rig(1, 1)
-        nc.sync.dma_start(gain_sb[:], gain.rearrange("(g p t) -> p g t", g=2, t=PACK))
         w3_raw.append(load_weight(w3, 0, 0))
         w3_raw.append(load_weight(w3, 1, 0))
         load_target(0)
@@ -178,7 +178,7 @@ def tile_list_playground_hazard_misfit_kernel(
 
         def weigh(i):
             g, t = divmod(i, PACK)
-            acc = banks[g][t]
+            acc = banks[1][t]
             nc.tensor.matmul_mx(
                 out=acc[:],
                 lhsT=w2_codes[:, 2 * P * i : 2 * P * (i + 1)].bitcast(FP4X4),
@@ -202,7 +202,7 @@ def tile_list_playground_hazard_misfit_kernel(
             f_t[g, h] = ring.tile([P, 4, HALF], F32, name="f_t", tag="f_t", bufs=4)
             for c in range(4):
                 cols = slice(h * HALF + c * P, h * HALF + (c + 1) * P)
-                acc = banks[0 if (g, h) == (0, 0) else 1][c]
+                acc = banks[h][c]
                 for a in range(2):
                     codes, scales = w1_q[a, g]
                     nc.tensor.matmul_mx(
@@ -220,7 +220,7 @@ def tile_list_playground_hazard_misfit_kernel(
                 )
 
         cos_t = {}
-        scratch = [keep.tile([P, 2, HALF], F32, name="scratch%d" % u, align_bytes=64) for u in range(2)]
+        scratch = [w1_raw[1, 1][:, 2 * u : 2 * u + 2, :] for u in range(2)]
 
         def cosines(g, h):
             cos_t[g, h] = ring.tile([P, 4, HALF], F32, name="cos_t", tag="cos_t", bufs=3)

@@ -56,6 +56,10 @@ def tile_list_playground_hazard_misfit_kernel(
         nc.vector.memset(tab2_sc[:].bitcast(I32), 0)
         nc.vector.memset(zero[:], 0.0)
         nc.scalar.activation(zero_bias[:], zero[:], ACT.Sin)
+        for q in range(4):
+            nc.gpsimd.dma_start(tab_sc[32 * q : 32 * q + 8, :].bitcast(I32), tab_scales[:, 4 * q : 4 * q + 4, :].bitcast(I32))
+        for q in range(4):
+            nc.gpsimd.dma_start(tab2_sc[32 * q : 32 * q + 4, :].bitcast(I32), tab2_scales[0, 4 * q : 4 * q + 4, :].bitcast(I32))
         for page in pages:
             nc.gpsimd.memset(page[:], 0.0)
         make_identity(nc, ident[:])
@@ -95,14 +99,9 @@ def tile_list_playground_hazard_misfit_kernel(
         nc.sync.dma_start(tabs[1][:], tab_words[1].rearrange("p n i -> p (n i)").bitcast(I32))
         nc.sync.dma_start(offs2_sb[:], offs2)
         nc.sync.dma_start(pos_sb[:], pos1)
-        nc.sync.dma_start(gain_sb[:], gain.rearrange("(g p t) -> p g t", g=2, t=PACK))
         nc.sync.dma_start(w2_raw[:].bitcast(I32), w2_words[0].bitcast(I32))
         w1_raw[0, 0] = load_weight(w1, 0, 0)
-        for q in range(4):
-            nc.sync.dma_start(tab_sc[32 * q : 32 * q + 8, :].bitcast(I32), tab_scales[:, 4 * q : 4 * q + 4, :].bitcast(I32))
         w1_raw[1, 0] = load_weight(w1, 1, 0)
-        for q in range(4):
-            nc.sync.dma_start(tab2_sc[32 * q : 32 * q + 4, :].bitcast(I32), tab2_scales[0, 4 * q : 4 * q + 4, :].bitcast(I32))
         tab2 = big("tab2")
         nc.sync.dma_start(tab2[:], tab2_words[0].rearrange("p n i -> p (n i)").bitcast(I32))
         for q in range(4):
@@ -115,6 +114,7 @@ def tile_list_playground_hazard_misfit_kernel(
         load_rig(0, 1)
         load_rig(1, 0)
         load_rig(1, 1)
+        nc.sync.dma_start(gain_sb[:], gain.rearrange("(g p t) -> p g t", g=2, t=PACK))
         w3_raw.append(load_weight(w3, 0, 0))
         w3_raw.append(load_weight(w3, 1, 0))
         load_target(0)

import math
from contextlib import ExitStack

import concourse.mybir as mybir
from concourse.masks import make_identity

K, K2, H, N, S, NP, T = 1024, 512, 1024, 512, 1024, 512, 2048
FLOPS = 2 * (K * H * S + K2 * H * NP + H * N * S)

F32 = mybir.dt.float32
BF16 = mybir.dt.bfloat16
I32 = mybir.dt.int32
U32 = mybir.dt.uint32
U16 = mybir.dt.uint16
U8 = mybir.dt.uint8
FP8X4 = mybir.dt.float8_e4m3fn_x4
FP4X4 = mybir.dt.float4_e2m1fn_x4
ALU = mybir.AluOpType
ACT = mybir.ActivationFunctionType

P = 128
PACK = 4
PASS = P * PACK
HALF = 512
PAGES = 6


def tile_list_playground_hazard_misfit_kernel(
    tc, tab_words, tab_scales, offs, tab2_words, tab2_scales, offs2, pos1, w1, gain,
    w2_words, w2_scales, rig, wgs, w3, target, out,
):
    nc = tc.nc
    with ExitStack() as ctx:
        keep = ctx.enter_context(tc.tile_pool(name="keep", bufs=1))
        ring = ctx.enter_context(tc.tile_pool(name="ring", bufs=2))
        psum = ctx.enter_context(tc.psum_pool(name="psum", bufs=2))

        offs_sb = keep.tile([P, S // 16], U16, name="offs_sb")
        offs2_sb = keep.tile([P, NP // 16], U16, name="offs2_sb")
        pos_sb = keep.tile([P, NP // 16], U16, name="pos_sb")
        tab_sc = keep.tile([P, T], U8, name="tab_sc", align_bytes=64)
        tab2_sc = keep.tile([P, T], U8, name="tab2_sc", align_bytes=64)
        w2_sc_raw = keep.tile([P, H], U8, name="w2_sc_raw", align_bytes=64)
        w2_raw = keep.tile([P, 2 * H], U8, name="w2_raw", align_bytes=64)
        w2_codes = keep.tile([P, 2 * H], U8, name="w2_codes", align_bytes=64)
        w2_sc = keep.tile([P, H], U8, name="w2_sc", align_bytes=64)
        gain_sb = keep.tile([P, 2, PACK], F32, name="gain_sb")
        wgs_sb = keep.tile([P, PACK, NP], F32, name="wgs_sb")
        ident = keep.tile([P, P], F32, name="ident")
        zero = keep.tile([P, 1], F32, name="zero")
        zero_bias = keep.tile([P, 1], F32, name="zero_bias")
        pages = [keep.tile([P, S], F32, name="page%d" % i) for i in range(PAGES)]

        nc.gpsimd.memset(tab_sc[:].bitcast(I32), 0)
        nc.gpsimd.memset(w2_sc_raw[:].bitcast(I32), 0)
        nc.vector.memset(tab2_sc[:].bitcast(I32), 0)
        nc.vector.memset(zero[:], 0.0)
        nc.scalar.activation(zero_bias[:], zero[:], ACT.Sin)
        for q in range(4):
            nc.gpsimd.dma_start(tab_sc[32 * q : 32 * q + 8, :].bitcast(I32), tab_scales[:, 4 * q : 4 * q + 4, :].bitcast(I32))
        for q in range(4):
            nc.gpsimd.dma_start(tab2_sc[32 * q : 32 * q + 4, :].bitcast(I32), tab2_scales[0, 4 * q : 4 * q + 4, :].bitcast(I32))
        for page in pages:
            nc.gpsimd.memset(page[:], 0.0)
        make_identity(nc, ident[:])

        banks = [[psum.tile([P, HALF], F32, name="bank%d%d" % (h, t), bufs=1) for t in range(4)] for h in range(2)]

        def big(name):
            return ring.tile([P, T], I32, name=name, tag="big", bufs=3, align_bytes=64)

        def load_weight(w, a, c):
            raw = ring.tile([P, PACK, HALF], F32, name="w_raw", tag="w_raw", bufs=5, align_bytes=64)
            rows = w[a * PASS : (a + 1) * PASS, c * HALF : (c + 1) * HALF]
            nc.sync.dma_start(raw[:], rows.rearrange("(p i) c -> p i c", i=PACK))
            return raw

        rig_sb = {}

        def load_rig(g, u):
            tile = keep.tile([P, 2, NP], F32, name="rig%d%d" % (g, u))
            rows = rig[g * PASS : (g + 1) * PASS, :].rearrange("(p t) j -> p t j", t=PACK)
            nc.sync.dma_start(tile[:], rows[:, 2 * u : 2 * u + 2, :])
            rig_sb[g, u] = tile

        def load_target(h):
            view = ring.tile([P, 4, HALF], F32, name="target_sb", tag="w_raw", bufs=5, align_bytes=64)[:]
            nc.sync.dma_start(view, target[:, h * HALF : (h + 1) * HALF].rearrange("(q p) j -> p q j", p=P))
            target_sb[h] = view

        w1_raw = {}
        w3_raw = []
        target_sb = {}
        tabs = []
        nc.sync.dma_start(offs_sb[:], offs)
        tabs.append(big("tab0"))
        nc.sync.dma_start(tabs[0][:], tab_words[0].rearrange("p n i -> p (n i)").bitcast(I32))
        tabs.append(big("tab1"))
        nc.sync.dma_start(tabs[1][:], tab_words[1].rearrange("p n i -> p (n i)").bitcast(I32))
        nc.sync.dma_start(offs2_sb[:], offs2)
        nc.sync.dma_start(pos_sb[:], pos1)
        nc.sync.dma_start(w2_raw[:].bitcast(I32), w2_words[0].bitcast(I32))
        w1_raw[0, 0] = load_weight(w1, 0, 0)
        w1_raw[1, 0] = load_weight(w1, 1, 0)
        tab2 = big("tab2")
        nc.sync.dma_start(tab2[:], tab2_words[0].rearrange("p n i -> p (n i)").bitcast(I32))
        for q in range(4):
            nc.sync.dma_start(w2_sc_raw[32 * q : 32 * q + 4, :].bitcast(I32), w2_scales[0, 4 * q : 4 * q + 4, :].bitcast(I32))
        for q in (0, 2, 1, 3):
            nc.sync.dma_start(wgs_sb[32 * q : 32 * q + 32, :, :], wgs.rearrange("(p t) j -> p t j", t=PACK))
        w1_raw[0, 1] = load_weight(w1, 0, 1)
        w1_raw[1, 1] = load_weight(w1, 1, 1)
        load_rig(0, 0)
        load_rig(0, 1)
        load_rig(1, 0)
        load_rig(1, 1)
        nc.sync.dma_start(gain_sb[:], gain.rearrange("(g p t) -> p g t", g=2, t=PACK))
        w3_raw.append(load_weight(w3, 0, 0))
        w3_raw.append(load_weight(w3, 1, 0))
        load_target(0)
        load_target(1)

        v_codes = []
        for a in range(2):
            codes = keep.tile([P, S], I32, name="v_codes%d" % a, align_bytes=64)
            nc.vector.tensor_copy(codes[:].bitcast(U32), tabs[a][:].bitcast(U32).indirect(offs_sb[:]))
            v_codes.append(codes)
        v_sc = keep.tile([P, S], U8, name="v_sc", align_bytes=64)
        nc.vector.tensor_copy(v_sc[:], tab_sc[:].indirect(offs_sb[:]))
        v2_codes = keep.tile([P, NP], I32, name="v2_codes", align_bytes=64)
        nc.vector.tensor_copy(v2_codes[:].bitcast(U32), tab2[:].bitcast(U32).indirect(offs2_sb[:]))
        v2_sc = keep.tile([P, NP], U8, name="v2_sc", align_bytes=64)
        nc.vector.tensor_copy(v2_sc[:], tab2_sc[:].indirect(offs2_sb[:]))
        nc.vector.tensor_copy(
            w2_codes[:].rearrange("p (g t m b) -> p g t m b", g=2, t=PACK, b=2),
            w2_raw[:].rearrange("p (g m t b) -> p g t m b", g=2, t=PACK, b=2),
        )
        nc.vector.tensor_copy(
            w2_sc[:].rearrange("p (g t m) -> p g t m", g=2, t=PACK),
            w2_sc_raw[:].rearrange("p (g m t) -> p g t m", g=2, t=PACK),
        )

        def quantize(grouped):
            codes = ring.tile([P, HALF], I32, name="codes", tag="codes", bufs=6, align_bytes=64)
            scales = ring.tile([P, HALF], U8, name="scales", tag="scales", bufs=6, align_bytes=64)
            nc.vector.quantize_mx(out=codes[:].bitcast(FP8X4), scales=scales[:], in_=grouped[:])
            return codes, scales

        def grouped_tile():
            return ring.tile([P, PACK * HALF], BF16, name="grouped", tag="grouped", bufs=3, align_bytes=64)

        w1_q = {}

        def prepare_w1(g):
            for a in range(2):
                grouped = grouped_tile()
                nc.scalar.copy(
                    grouped[:].rearrange("p (c i t) -> p c t i", t=PACK, i=4),
                    w1_raw[a, g][:].rearrange("p t (c i) -> p c t i", i=4),
                )
                w1_q[a, g] = quantize(grouped)

        w3_q = {}

        def prepare_w3(g):
            raw = w3_raw[g]
            grouped = grouped_tile()
            nc.scalar.copy(
                grouped[:].rearrange("p (c i t) -> p c t i", t=PACK, i=4),
                raw[:].rearrange("p t (c i) -> p c t i", i=4),
            )
            w3_q[g] = quantize(grouped)

        def page_of(i):
            return pages[i] if i < PAGES else pages[PAGES + 3 - i]

        weighted = {}

        def weigh(i):
            g, t = divmod(i, PACK)
            acc = banks[1][t]
            nc.tensor.matmul_mx(
                out=acc[:],
                lhsT=w2_codes[:, 2 * P * i : 2 * P * (i + 1)].bitcast(FP4X4),
                lhsT_scale=w2_sc[:, P * i : P * (i + 1)],
                rhs=v2_codes[:].bitcast(FP8X4),
                rhs_scale=v2_sc[:],
                start=True,
                stop=True,
            )
            if t == 0:
                weighted[g] = big("b%d" % g)[:].bitcast(F32).rearrange("p (t j) -> p t j", t=PACK)
            nc.vector.tensor_tensor(weighted[g][:, t, :], acc[:], wgs_sb[:, t, :], ALU.mult)

        def place(i):
            g, t = divmod(i, PACK)
            nc.vector.tensor_tensor(page_of(i)[:].indirect(pos_sb[:]), weighted[g][:, t, :], rig_sb[g, t // 2][:, t % 2, :], ALU.mult)

        f_t = {}

        def products(g, h):
            f_t[g, h] = ring.tile([P, 4, HALF], F32, name="f_t", tag="f_t", bufs=4)
            for c in range(4):
                cols = slice(h * HALF + c * P, h * HALF + (c + 1) * P)
                acc = banks[h][c]
                for a in range(2):
                    codes, scales = w1_q[a, g]
                    nc.tensor.matmul_mx(
                        out=acc[:],
                        lhsT=v_codes[a][:, cols].bitcast(FP8X4),
                        lhsT_scale=v_sc[4 * a : P, cols],
                        rhs=codes[:].bitcast(FP8X4),
                        rhs_scale=scales[:],
                        start=(a == 0),
                        stop=(a == 1),
                    )
                nc.scalar.copy(
                    f_t[g, h][:, c, :].rearrange("p (t m) -> p t m", t=PACK),
                    acc[:].rearrange("p (m t) -> p t m", t=PACK),
                )

        cos_t = {}
        scratch = [w1_raw[1, 1][:, 2 * u : 2 * u + 2, :] for u in range(2)]

        def cosines(g, h):
            cos_t[g, h] = ring.tile([P, 4, HALF], F32, name="cos_t", tag="cos_t", bufs=3)
            for u in range(2):
                nc.scalar.activation(scratch[u][:], f_t[g, h][:, 2 * u : 2 * u + 2, :], ACT.Abs, bias=zero_bias[:])
            for u in range(2):
                nc.scalar.activation(cos_t[g, h][:, 2 * u : 2 * u + 2, :], scratch[u][:], ACT.Sin, bias=math.pi / 2, scale=-1.0)

        z_rows = {}

        def combine(i, h):
            g, t = divmod(i, PACK)
            if t == 0:
                z_rows[g, h] = ring.tile([P, PACK, HALF], BF16, name="z_rows", tag="z_rows", bufs=4)
            total = banks[h][t]
            for c in range(4):
                for n, term in enumerate((cos_t[g, h], f_t[g, h])):
                    nc.tensor.matmul(
                        total[:, c * P : (c + 1) * P],
                        lhsT=term[:, c, t * P : (t + 1) * P],
                        rhs=ident[:],
                        start=(n == 0),
                        stop=(n == 1),
                        is_transpose=True,
                    )
            nc.vector.scalar_tensor_tensor(
                out=z_rows[g, h][:, t, :],
                in0=total[:],
                scalar=gain_sb[:, g, t : t + 1],
                in1=page_of(i)[:, h * HALF : (h + 1) * HALF],
                op0=ALU.mult,
                op1=ALU.add,
            )

        z_q = {}

        def prepare_z(g, h):
            if g == 0:
                grouped = scratch[h][:].rearrange("p c r -> p (c r)").bitcast(BF16)
            else:
                grouped = grouped_tile()
            nc.scalar.copy(
                grouped[:].rearrange("p (c i t) -> p c t i", t=PACK, i=4),
                z_rows[g, h][:].rearrange("p t (c i) -> p c t i", i=4),
            )
            z_q[g, h] = quantize(grouped)

        diffs = {}

        def misfit(q, h):
            acc = banks[h][q]
            for g in (h, 1 - h):
                w_codes, w_scales = w3_q[g]
                z_codes, z_scales = z_q[g, h]
                nc.tensor.matmul_mx(
                    out=acc[:],
                    lhsT=w_codes[:, P * q : P * (q + 1)].bitcast(FP8X4),
                    lhsT_scale=w_scales[:, P * q : P * (q + 1)],
                    rhs=z_codes[:].bitcast(FP8X4),
                    rhs_scale=z_scales[:],
                    start=(g == h),
                    stop=(g != h),
                )
            if q == 0:
                diffs[h] = ring.tile([P, 4, HALF], F32, name="diff", tag="f_t", bufs=4)
            diff = diffs[h][:, q, :]
            nc.vector.tensor_tensor(diff, acc[:], target_sb[h][:, q, :], ALU.subtract)
            nc.scalar.activation(diff, diff, ACT.Square)
            nc.sync.dma_start(out[q * P : (q + 1) * P, h * HALF : (h + 1) * HALF], diff)

        prepare_w1(0)
        prepare_w1(1)
        for i in range(8):
            weigh(i)
        for i in range(PAGES):
            place(i)
        products(0, 0)
        products(0, 1)
        cosines(0, 0)
        products(1, 0)
        products(1, 1)
        cosines(0, 1)
        cosines(1, 0)
        cosines(1, 1)
        for h in range(2):
            for t in range(PACK):
                combine(t, h)
        for i in range(PAGES, 8):
            place(i)
        for h in range(2):
            for t in range(PACK):
                combine(PACK + t, h)
        for g in range(2):
            prepare_w3(g)
            prepare_z(0, g)
        prepare_z(1, 0)
        prepare_z(1, 1)
        for h in range(2):
            for q in range(4):
                misfit(q, h)
